import numpy as np
import ml_dtypes


def mxq(x, axis, fmt="e4m3"):
    dtype, down = {"e4m3": (ml_dtypes.float8_e4m3fn, 7), "e5m2": (ml_dtypes.float8_e5m2, 14)}[fmt]
    v = np.moveaxis(np.asarray(x, np.float32).astype(ml_dtypes.bfloat16).astype(np.float64), axis, -1)
    blocks = v.reshape(v.shape[:-1] + (-1, 32))
    amax = np.abs(blocks).max(-1, keepdims=True)
    byte = np.maximum(np.where(amax > 0, np.frexp(amax)[1] - 1 + 127, 0) - down, 1)
    scale = np.exp2(byte - 127.0)
    codes = (blocks / scale).astype(np.float32).astype(dtype).astype(np.float64)
    return np.moveaxis((codes * scale).reshape(v.shape), -1, axis)


WIDE = False


def mx_kscale(k):
    if not WIDE:
        return np.ones(k)
    levels = np.array([10, -10, 5, -5, 0])
    if k % 512:
        return np.exp2(np.random.permutation(np.resize(levels, k // 32))).repeat(32)
    a = np.empty((k // 512, 16))
    for p in range(k // 512):
        a[p, :8] = np.random.permutation(np.resize(levels, 8))
        for g in range(8):
            far = levels[np.abs(levels - a[p, g]) >= 10]
            a[p, g + 8] = far[np.random.randint(len(far))]
    return np.exp2(a.ravel()).repeat(32)


def f64(x):
    return np.asarray(x).astype(np.float64)


def striped(idx):
    return np.tile(idx.reshape(-1, 16).T, (8, 1)).astype(np.uint16)


def unstriped(offs):
    return offs[:16].T.reshape(-1).astype(np.int64)


def pack_weight(w):
    k, n = w.shape
    w = f64(np.asarray(w, np.float32).astype(ml_dtypes.bfloat16)).reshape(k // 32, 32, n)
    amax = np.abs(w).max(1)
    byte = np.clip(np.where(amax > 0, np.frexp(amax)[1] - 1 + 127 - 7, 1), 1, 254)
    scaled = (w * np.exp2(127.0 - byte)[:, None, :]).reshape(k, n).astype(np.float32)
    words = np.ascontiguousarray(scaled.reshape(k // 512, 128, 4, n).transpose(0, 1, 3, 2)).astype(ml_dtypes.float8_e4m3fn).view(np.uint8)
    return words, np.ascontiguousarray(byte.astype(np.uint8).reshape(k // 512, 16, n))


def unpack_weight(words, scales):
    g, p, n, _ = words.shape
    vals = np.ascontiguousarray(words).view(ml_dtypes.float8_e4m3fn).astype(np.float64) * np.repeat(np.exp2(scales.astype(np.float64) - 127.0), 8, axis=1)[..., None]
    return vals.transpose(0, 1, 3, 2).reshape(g * 512, n)


K, T, E, C, N = 512, 512, 4, 128, 128


def by_expert(wq, xq):
    return np.concatenate([wq[e].T @ xq[:, e * C:(e + 1) * C] for e in range(E)], axis=1)


def setup_inputs():
    n = np.random.standard_normal
    s = mx_kscale(K)[:, None]
    packed = [pack_weight(m) for m in n((E, K, N)) / np.sqrt(K) / s[None]]
    return {
        "xT": (n((K, T)) * s).astype(np.float32),
        "w_words": np.stack([m[0] for m in packed]),
        "w_scales": np.stack([m[1] for m in packed]),
        "gate": np.tile(np.random.uniform(0.2, 1.0, E * C), (N, 1)).astype(np.float32),
        "offs": striped(np.random.permutation(T)[:E * C]),
    }


def reference(xT, w_words, w_scales, gate, offs):
    idx = unstriped(offs)
    xq = mxq(f64(xT)[:, idx], 0, "e4m3")
    w = np.stack([unpack_weight(w_words[e], w_scales[e]) for e in range(E)])
    y = by_expert(w, xq)
    out = np.zeros((N, T))
    out[:, idx] = f64(gate) * y
    return out

@@ -1,0 +1,126 @@
+import concourse.mybir as mybir
+
+F32 = mybir.dt.float32
+BF16 = mybir.dt.bfloat16
+I32 = mybir.dt.int32
+U32 = mybir.dt.uint32
+U16 = mybir.dt.uint16
+U8 = mybir.dt.uint8
+FP8X4 = mybir.dt.float8_e4m3fn_x4
+MULT = mybir.AluOpType.mult
+
+P = 128
+K, T, E, C, N = 512, 512, 4, 128, 128
+S = E * C
+FLOPS = 2 * K * S * N
+PARTS = (256,128,128)
+GROUPS = ((0,1),(1,3))
+LOADS = ((0,0,256),(0,256,512),(1,0,256),(1,256,512))
+
+def tile_routed_moe_kernel(tc, xT, w_words, w_scales, gate, offs, out):
+    nc = tc.nc
+    with (
+        tc.tile_pool(name="held", bufs=1) as held,
+        tc.psum_pool(name="psum", bufs=1) as psum,
+    ):
+        lists = held.tile([P, S // 16], U16, name="lists")
+        warm = held.tile([P, 8], F32, name="warm")
+        warm_out = held.tile([P, 8], F32, name="warm_out")
+        planes = held.tile([P, N], U8, name="planes", align_bytes=64)
+        raw = [held.tile([P, 2, T], F32, name=f"raw{u}", align_bytes=64) for u in range(2)]
+        pair = [held.tile([P, T, 2], BF16, name=f"pair{u}", align_bytes=64) for u in range(2)]
+        words = held.tile([P, E, 4 * N], U8, name="words", align_bytes=64)
+        gates = held.tile([P, S], F32, name="gates", align_bytes=64)
+        result = held.tile([P, T], F32, name="result", align_bytes=64)
+
+        nc.vector.memset(planes[:].bitcast(I32), 0)
+        nc.gpsimd.memset(warm[:], 0.0)
+        nc.scalar.copy(warm_out[:], warm[:])
+
+        rows = xT.rearrange("(p t) n -> p t n", t=4)
+        for i, (u, a, b) in enumerate(LOADS):
+            nc.sync.dma_start(raw[u][:, :, a:b], rows[:, 2 * u : 2 * u + 2, a:b])
+            if i == 0:
+                nc.sync.dma_start(lists[:], offs)
+        for q in range(4):
+            nc.sync.dma_start(
+                planes[32 * q : 32 * q + 16, :].bitcast(I32),
+                w_scales[:, 0, 4 * q : 4 * q + 4, :].bitcast(I32),
+            )
+        nc.sync.dma_start(words[:].bitcast(I32), w_words.rearrange("e a p n r -> p (e a) (n r)").bitcast(I32))
+        nc.sync.dma_start(gates[:], gate)
+
+        def cast(u, a, b, engine):
+            dst = pair[u][:, a:b, :]
+            src = raw[u][:, :, a:b].rearrange("p t n -> p n t")
+            if engine == "v":
+                nc.vector.tensor_copy(dst, src)
+            else:
+                nc.scalar.copy(dst, src)
+
+        starts = [sum(PARTS[:h]) for h in range(len(PARTS))]
+        mixed = [held.tile([P, n, 4], BF16, name=f"mixed{h}", align_bytes=64) for h, n in enumerate(PARTS)]
+        codes = [held.tile([P, n], U32, name=f"codes{h}", align_bytes=64) for h, n in enumerate(PARTS)]
+        scales = [held.tile([P, n], U8, name=f"scales{h}", align_bytes=64) for h, n in enumerate(PARTS)]
+        sums = [psum.tile([P, n], F32, name=f"sums{h}") for h, n in enumerate(PARTS)]
+        gated = [held.tile([P, sum(PARTS[g[0]:g[1]])], F32, name=f"gated{i}", align_bytes=64) for i, g in enumerate(GROUPS)]
+
+        def gather(u, h):
+            window = pair[u][:].rearrange("p n t -> p (n t)").bitcast(U32)
+            slots = lists[:, starts[h] // 16 : (starts[h] + PARTS[h]) // 16]
+            dst = mixed[h][:].rearrange("p n t -> p (n t)").bitcast(U32).rearrange("p (n u) -> p n u", u=2)
+            nc.vector.tensor_copy(dst[:, :, u], window.indirect(slots))
+
+        def quantise(h):
+            nc.vector.quantize_mx(out=codes[h][:].bitcast(FP8X4), scales=scales[h][:], in_=mixed[h][:].rearrange("p n t -> p (n t)"))
+
+        def multiply(h):
+            for i in range(PARTS[h] // C):
+                e = starts[h] // C + i
+                cols = slice(i * C, (i + 1) * C)
+                nc.tensor.matmul_mx(
+                    out=sums[h][:, cols],
+                    lhsT=words[:, e, :].bitcast(FP8X4),
+                    lhsT_scale=planes[4 * e : P, :],
+                    rhs=codes[h][:, cols].bitcast(FP8X4),
+                    rhs_scale=scales[h][:, cols],
+                    start=True,
+                    stop=True,
+                )
+
+        def leave(h):
+            g = [i for i, (a, b) in enumerate(GROUPS) if a <= h < b][0]
+            at = starts[h] - starts[GROUPS[g][0]]
+            dst = gated[g][:, at : at + PARTS[h]]
+            nc.vector.tensor_tensor(dst, sums[h][:], gates[:, starts[h] : starts[h] + PARTS[h]], MULT)
+
+        def scatter(g):
+            a = starts[GROUPS[g][0]]
+            b = a + sum(PARTS[GROUPS[g][0] : GROUPS[g][1]])
+            slots = lists[:, a // 16 : b // 16]
+            nc.vector.tensor_copy(result[:].indirect(slots), gated[g][:])
+
+        cast(0, 0, 256, "v")
+        cast(0, 256, 416, "v")
+        cast(0, 416, 512, "s")
+        gather(0, 0)
+        gather(0, 1)
+        gather(0, 2)
+        cast(1, 0, 256, "s")
+        cast(1, 256, 448, "s")
+        cast(1, 448, 512, "v")
+        gather(1, 0)
+        gather(1, 1)
+        quantise(0)
+        multiply(0)
+        gather(1, 2)
+        quantise(1)
+        multiply(1)
+        leave(0)
+        quantise(2)
+        multiply(2)
+        scatter(0)
+        leave(1)
+        leave(2)
+        scatter(1)
+        nc.sync.dma_start(out, result[:])

@@ -92,13 +92,13 @@ def tile_routed_moe_kernel(tc, xT, w_words, w_scales, gate, offs, out):
             g = [i for i, (a, b) in enumerate(GROUPS) if a <= h < b][0]
             at = starts[h] - starts[GROUPS[g][0]]
             dst = gated[g][:, at : at + PARTS[h]]
-            nc.vector.tensor_tensor(dst, sums[h][:], gates[:, starts[h] : starts[h] + PARTS[h]], MULT)
+            nc.scalar.copy(dst, sums[h][:])
 
         def scatter(g):
             a = starts[GROUPS[g][0]]
             b = a + sum(PARTS[GROUPS[g][0] : GROUPS[g][1]])
             slots = lists[:, a // 16 : b // 16]
-            nc.vector.tensor_copy(result[:].indirect(slots), gated[g][:])
+            nc.vector.tensor_tensor(result[:].indirect(slots), gated[g][:], gates[:, a:b], MULT)
 
         cast(0, 0, 256, "v")
         cast(0, 256, 416, "v")

@@ -13,42 +13,48 @@ P = 128
 K, T, E, C, N = 512, 512, 4, 128, 128
 S = E * C
 FLOPS = 2 * K * S * N
-PARTS = (256,128,128)
-GROUPS = ((0,1),(1,3))
-LOADS = ((0,0,256),(0,256,512),(1,0,256),(1,256,512))
+
+PARTS = ((0, 128), (128, 384), (384, 512))
+
 
 def tile_routed_moe_kernel(tc, xT, w_words, w_scales, gate, offs, out):
     nc = tc.nc
     with (
         tc.tile_pool(name="held", bufs=1) as held,
+        tc.tile_pool(name="ring", bufs=2) as ring,
         tc.psum_pool(name="psum", bufs=1) as psum,
     ):
         lists = held.tile([P, S // 16], U16, name="lists")
         warm = held.tile([P, 8], F32, name="warm")
         warm_out = held.tile([P, 8], F32, name="warm_out")
         planes = held.tile([P, N], U8, name="planes", align_bytes=64)
-        raw = [held.tile([P, 2, T], F32, name=f"raw{u}", align_bytes=64) for u in range(2)]
-        pair = [held.tile([P, T, 2], BF16, name=f"pair{u}", align_bytes=64) for u in range(2)]
         words = held.tile([P, E, 4 * N], U8, name="words", align_bytes=64)
         gates = held.tile([P, S], F32, name="gates", align_bytes=64)
-        result = held.tile([P, T], F32, name="result", align_bytes=64)
+        result = held.tile([P, 768], F32, name="result", align_bytes=64)
+        raw = [held.tile([P, 2, T], F32, name=f"raw{u}", align_bytes=64) for u in range(2)]
+        pair = [held.tile([P, T, 2], BF16, name=f"pair{u}", align_bytes=64) for u in range(2)]
+        codes = [held.tile([P, b - a], U32, name=f"codes{a}", align_bytes=64) for a, b in PARTS]
+        scales = [held.tile([P, b - a], U8, name=f"scales{a}", align_bytes=64) for a, b in PARTS]
+        sums = [psum.tile([P, b - a], F32, name=f"sums{a}") for a, b in PARTS]
+        slot_sums = held.tile([P, S], F32, name="slot_sums", align_bytes=64)
 
         nc.vector.memset(planes[:].bitcast(I32), 0)
         nc.gpsimd.memset(warm[:], 0.0)
         nc.scalar.copy(warm_out[:], warm[:])
 
         rows = xT.rearrange("(p t) n -> p t n", t=4)
-        for i, (u, a, b) in enumerate(LOADS):
+
+        def load(u, a, b):
             nc.sync.dma_start(raw[u][:, :, a:b], rows[:, 2 * u : 2 * u + 2, a:b])
-            if i == 0:
-                nc.sync.dma_start(lists[:], offs)
-        for q in range(4):
-            nc.sync.dma_start(
-                planes[32 * q : 32 * q + 16, :].bitcast(I32),
-                w_scales[:, 0, 4 * q : 4 * q + 4, :].bitcast(I32),
-            )
-        nc.sync.dma_start(words[:].bitcast(I32), w_words.rearrange("e a p n r -> p (e a) (n r)").bitcast(I32))
-        nc.sync.dma_start(gates[:], gate)
+
+        def load_rest():
+            for q in range(4):
+                nc.sync.dma_start(
+                    planes[32 * q : 32 * q + 16, :].bitcast(I32),
+                    w_scales[:, 0, 4 * q : 4 * q + 4, :].bitcast(I32),
+                )
+            nc.sync.dma_start(words[:].bitcast(I32), w_words.rearrange("e a p n r -> p (e a) (n r)").bitcast(I32))
+            nc.sync.dma_start(gates[:], gate)
 
         def cast(u, a, b, engine):
             dst = pair[u][:, a:b, :]
@@ -58,26 +64,25 @@ def tile_routed_moe_kernel(tc, xT, w_words, w_scales, gate, offs, out):
             else:
                 nc.scalar.copy(dst, src)
 
-        starts = [sum(PARTS[:h]) for h in range(len(PARTS))]
-        mixed = [held.tile([P, n, 4], BF16, name=f"mixed{h}", align_bytes=64) for h, n in enumerate(PARTS)]
-        codes = [held.tile([P, n], U32, name=f"codes{h}", align_bytes=64) for h, n in enumerate(PARTS)]
-        scales = [held.tile([P, n], U8, name=f"scales{h}", align_bytes=64) for h, n in enumerate(PARTS)]
-        sums = [psum.tile([P, n], F32, name=f"sums{h}") for h, n in enumerate(PARTS)]
-        gated = [held.tile([P, sum(PARTS[g[0]:g[1]])], F32, name=f"gated{i}", align_bytes=64) for i, g in enumerate(GROUPS)]
+        mixed = {}
 
         def gather(u, h):
+            a, b = PARTS[h]
+            if h not in mixed:
+                mixed[h] = ring.tile([P, b - a, 4], BF16, name="mixed", align_bytes=64)
             window = pair[u][:].rearrange("p n t -> p (n t)").bitcast(U32)
-            slots = lists[:, starts[h] // 16 : (starts[h] + PARTS[h]) // 16]
             dst = mixed[h][:].rearrange("p n t -> p (n t)").bitcast(U32).rearrange("p (n u) -> p n u", u=2)
-            nc.vector.tensor_copy(dst[:, :, u], window.indirect(slots))
+            nc.vector.tensor_copy(dst[:, :, u], window.indirect(lists[:, a // 16 : b // 16]))
 
         def quantise(h):
-            nc.vector.quantize_mx(out=codes[h][:].bitcast(FP8X4), scales=scales[h][:], in_=mixed[h][:].rearrange("p n t -> p (n t)"))
+            nc.vector.quantize_mx(
+                out=codes[h][:].bitcast(FP8X4), scales=scales[h][:], in_=mixed[h][:].rearrange("p n t -> p (n t)")
+            )
 
         def multiply(h):
-            for i in range(PARTS[h] // C):
-                e = starts[h] // C + i
-                cols = slice(i * C, (i + 1) * C)
+            a, b = PARTS[h]
+            for e in range(a // C, b // C):
+                cols = slice(e * C - a, (e + 1) * C - a)
                 nc.tensor.matmul_mx(
                     out=sums[h][:, cols],
                     lhsT=words[:, e, :].bitcast(FP8X4),
@@ -87,40 +92,37 @@ def tile_routed_moe_kernel(tc, xT, w_words, w_scales, gate, offs, out):
                     start=True,
                     stop=True,
                 )
+            nc.scalar.copy(slot_sums[:, a:b], sums[h][:])
 
-        def leave(h):
-            g = [i for i, (a, b) in enumerate(GROUPS) if a <= h < b][0]
-            at = starts[h] - starts[GROUPS[g][0]]
-            dst = gated[g][:, at : at + PARTS[h]]
-            nc.scalar.copy(dst, sums[h][:])
+        def scatter(a, b):
+            nc.vector.tensor_tensor(
+                result[:].indirect(lists[:, a // 16 : b // 16]), slot_sums[:, a:b], gates[:, a:b], MULT
+            )
 
-        def scatter(g):
-            a = starts[GROUPS[g][0]]
-            b = a + sum(PARTS[GROUPS[g][0] : GROUPS[g][1]])
-            slots = lists[:, a // 16 : b // 16]
-            nc.vector.tensor_tensor(result[:].indirect(slots), gated[g][:], gates[:, a:b], MULT)
-
+        load(0, 0, 256)
+        nc.sync.dma_start(lists[:], offs)
+        load(0, 256, 512)
+        load(1, 0, 256)
+        load(1, 256, 512)
+        load_rest()
         cast(0, 0, 256, "v")
         cast(0, 256, 416, "v")
         cast(0, 416, 512, "s")
-        gather(0, 0)
-        gather(0, 1)
-        gather(0, 2)
         cast(1, 0, 256, "s")
-        cast(1, 256, 448, "s")
-        cast(1, 448, 512, "v")
+        cast(1, 256, 384, "s")
+        gather(0, 0)
+        cast(1, 384, 512, "v")
+        gather(0, 1)
         gather(1, 0)
         gather(1, 1)
         quantise(0)
         multiply(0)
+        gather(0, 2)
         gather(1, 2)
         quantise(1)
         multiply(1)
-        leave(0)
         quantise(2)
         multiply(2)
-        scatter(0)
-        leave(1)
-        leave(2)
-        scatter(1)
-        nc.sync.dma_start(out, result[:])
+        scatter(0, 128)
+        scatter(128, 512)
+        nc.sync.dma_start(out, result[:, 0:T])

@@ -14,7 +14,7 @@ K, T, E, C, N = 512, 512, 4, 128, 128
 S = E * C
 FLOPS = 2 * K * S * N
 
-PARTS = ((0, 128), (128, 384), (384, 512))
+PARTS = ((0, 256), (256, 384), (384, 512))
 
 
 def tile_routed_moe_kernel(tc, xT, w_words, w_scales, gate, offs, out):
@@ -30,7 +30,7 @@ def tile_routed_moe_kernel(tc, xT, w_words, w_scales, gate, offs, out):
         planes = held.tile([P, N], U8, name="planes", align_bytes=64)
         words = held.tile([P, E, 4 * N], U8, name="words", align_bytes=64)
         gates = held.tile([P, S], F32, name="gates", align_bytes=64)
-        result = held.tile([P, 768], F32, name="result", align_bytes=64)
+        result = held.tile([P, 512], F32, name="result", align_bytes=64)
         raw = [held.tile([P, 2, T], F32, name=f"raw{u}", align_bytes=64) for u in range(2)]
         pair = [held.tile([P, T, 2], BF16, name=f"pair{u}", align_bytes=64) for u in range(2)]
         codes = [held.tile([P, b - a], U32, name=f"codes{a}", align_bytes=64) for a, b in PARTS]
@@ -100,16 +100,18 @@ def tile_routed_moe_kernel(tc, xT, w_words, w_scales, gate, offs, out):
             )
 
         load(0, 0, 256)
+        load(0, 256, 384)
+        load(0, 384, 512)
         nc.sync.dma_start(lists[:], offs)
-        load(0, 256, 512)
-        load(1, 0, 256)
-        load(1, 256, 512)
+        load(1, 0, 128)
+        load(1, 128, 384)
+        load(1, 384, 512)
         load_rest()
         cast(0, 0, 256, "v")
-        cast(0, 256, 416, "v")
-        cast(0, 416, 512, "s")
-        cast(1, 0, 256, "s")
-        cast(1, 256, 384, "s")
+        cast(0, 256, 384, "s")
+        cast(0, 384, 512, "v")
+        cast(1, 0, 128, "s")
+        cast(1, 128, 384, "s")
         gather(0, 0)
         cast(1, 384, 512, "v")
         gather(0, 1)
@@ -123,6 +125,6 @@ def tile_routed_moe_kernel(tc, xT, w_words, w_scales, gate, offs, out):
         multiply(1)
         quantise(2)
         multiply(2)
-        scatter(0, 128)
-        scatter(128, 512)
+        scatter(0, 256)
+        scatter(256, 512)
         nc.sync.dma_start(out, result[:, 0:T])

import concourse.mybir as mybir

F32 = mybir.dt.float32
BF16 = mybir.dt.bfloat16
I32 = mybir.dt.int32
U32 = mybir.dt.uint32
U16 = mybir.dt.uint16
U8 = mybir.dt.uint8
FP8X4 = mybir.dt.float8_e4m3fn_x4
MULT = mybir.AluOpType.mult

P = 128
K, T, E, C, N = 512, 512, 4, 128, 128
S = E * C
FLOPS = 2 * K * S * N

PARTS = ((0, 256), (256, 384), (384, 512))


def tile_routed_moe_kernel(tc, xT, w_words, w_scales, gate, offs, out):
    nc = tc.nc
    with (
        tc.tile_pool(name="held", bufs=1) as held,
        tc.tile_pool(name="ring", bufs=2) as ring,
        tc.psum_pool(name="psum", bufs=1) as psum,
    ):
        lists = held.tile([P, S // 16], U16, name="lists")
        warm = held.tile([P, 8], F32, name="warm")
        warm_out = held.tile([P, 8], F32, name="warm_out")
        planes = held.tile([P, N], U8, name="planes", align_bytes=64)
        words = held.tile([P, E, 4 * N], U8, name="words", align_bytes=64)
        gates = held.tile([P, S], F32, name="gates", align_bytes=64)
        result = held.tile([P, 512], F32, name="result", align_bytes=64)
        raw = [held.tile([P, 2, T], F32, name=f"raw{u}", align_bytes=64) for u in range(2)]
        pair = [held.tile([P, T, 2], BF16, name=f"pair{u}", align_bytes=64) for u in range(2)]
        codes = [held.tile([P, b - a], U32, name=f"codes{a}", align_bytes=64) for a, b in PARTS]
        scales = [held.tile([P, b - a], U8, name=f"scales{a}", align_bytes=64) for a, b in PARTS]
        sums = [psum.tile([P, b - a], F32, name=f"sums{a}") for a, b in PARTS]
        slot_sums = held.tile([P, S], F32, name="slot_sums", align_bytes=64)

        nc.vector.memset(planes[:].bitcast(I32), 0)
        nc.gpsimd.memset(warm[:], 0.0)
        nc.scalar.copy(warm_out[:], warm[:])

        rows = xT.rearrange("(p t) n -> p t n", t=4)

        def load(u, a, b):
            nc.sync.dma_start(raw[u][:, :, a:b], rows[:, 2 * u : 2 * u + 2, a:b])

        def load_rest():
            for q in range(4):
                nc.sync.dma_start(
                    planes[32 * q : 32 * q + 16, :].bitcast(I32),
                    w_scales[:, 0, 4 * q : 4 * q + 4, :].bitcast(I32),
                )
            nc.sync.dma_start(words[:].bitcast(I32), w_words.rearrange("e a p n r -> p (e a) (n r)").bitcast(I32))
            nc.sync.dma_start(gates[:], gate)

        def cast(u, a, b, engine):
            dst = pair[u][:, a:b, :]
            src = raw[u][:, :, a:b].rearrange("p t n -> p n t")
            if engine == "v":
                nc.vector.tensor_copy(dst, src)
            else:
                nc.scalar.copy(dst, src)

        mixed = {}

        def gather(u, h):
            a, b = PARTS[h]
            if h not in mixed:
                mixed[h] = ring.tile([P, b - a, 4], BF16, name="mixed", align_bytes=64)
            window = pair[u][:].rearrange("p n t -> p (n t)").bitcast(U32)
            dst = mixed[h][:].rearrange("p n t -> p (n t)").bitcast(U32).rearrange("p (n u) -> p n u", u=2)
            nc.vector.tensor_copy(dst[:, :, u], window.indirect(lists[:, a // 16 : b // 16]))

        def quantise(h):
            nc.vector.quantize_mx(
                out=codes[h][:].bitcast(FP8X4), scales=scales[h][:], in_=mixed[h][:].rearrange("p n t -> p (n t)")
            )

        def multiply(h):
            a, b = PARTS[h]
            for e in range(a // C, b // C):
                cols = slice(e * C - a, (e + 1) * C - a)
                nc.tensor.matmul_mx(
                    out=sums[h][:, cols],
                    lhsT=words[:, e, :].bitcast(FP8X4),
                    lhsT_scale=planes[4 * e : P, :],
                    rhs=codes[h][:, cols].bitcast(FP8X4),
                    rhs_scale=scales[h][:, cols],
                    start=True,
                    stop=True,
                )
            nc.scalar.copy(slot_sums[:, a:b], sums[h][:])

        def scatter(a, b):
            nc.vector.tensor_tensor(
                result[:].indirect(lists[:, a // 16 : b // 16]), slot_sums[:, a:b], gates[:, a:b], MULT
            )

        load(0, 0, 256)
        load(0, 256, 384)
        load(0, 384, 512)
        nc.sync.dma_start(lists[:], offs)
        load(1, 0, 128)
        load(1, 128, 384)
        load(1, 384, 512)
        load_rest()
        cast(0, 0, 256, "v")
        cast(0, 256, 384, "s")
        cast(0, 384, 512, "v")
        cast(1, 0, 128, "s")
        cast(1, 128, 384, "s")
        gather(0, 0)
        cast(1, 384, 512, "v")
        gather(0, 1)
        gather(1, 0)
        gather(1, 1)
        quantise(0)
        multiply(0)
        gather(0, 2)
        gather(1, 2)
        quantise(1)
        multiply(1)
        quantise(2)
        multiply(2)
        scatter(0, 256)
        scatter(256, 512)
        nc.sync.dma_start(out, result[:, 0:T])
